import numpy as np
import ml_dtypes


def mxq(x, axis, fmt="e4m3"):
    dtype, down = {"e4m3": (ml_dtypes.float8_e4m3fn, 7), "e5m2": (ml_dtypes.float8_e5m2, 14)}[fmt]
    v = np.moveaxis(np.asarray(x, np.float32).astype(ml_dtypes.bfloat16).astype(np.float64), axis, -1)
    blocks = v.reshape(v.shape[:-1] + (-1, 32))
    amax = np.abs(blocks).max(-1, keepdims=True)
    byte = np.maximum(np.where(amax > 0, np.frexp(amax)[1] - 1 + 127, 0) - down, 1)
    scale = np.exp2(byte - 127.0)
    codes = (blocks / scale).astype(np.float32).astype(dtype).astype(np.float64)
    return np.moveaxis((codes * scale).reshape(v.shape), -1, axis)


WIDE = False


def mx_kscale(k):
    if not WIDE:
        return np.ones(k)
    levels = np.array([10, -10, 5, -5, 0])
    if k % 512:
        return np.exp2(np.random.permutation(np.resize(levels, k // 32))).repeat(32)
    a = np.empty((k // 512, 16))
    for p in range(k // 512):
        a[p, :8] = np.random.permutation(np.resize(levels, 8))
        for g in range(8):
            far = levels[np.abs(levels - a[p, g]) >= 10]
            a[p, g + 8] = far[np.random.randint(len(far))]
    return np.exp2(a.ravel()).repeat(32)


def f64(x):
    return np.asarray(x).astype(np.float64)


def striped(idx):
    return np.tile(idx.reshape(-1, 16).T, (8, 1)).astype(np.uint16)


def unstriped(offs):
    return offs[:16].T.reshape(-1).astype(np.int64)


E2M1 = np.array([0.0, 0.5, 1.0, 1.5, 2.0, 3.0, 4.0, 6.0, -0.0, -0.5, -1.0, -1.5, -2.0, -3.0, -4.0, -6.0])


def pack_weight(w, fmt):
    k, n = w.shape
    w = f64(np.asarray(w, np.float32).astype(ml_dtypes.bfloat16)).reshape(k // 32, 32, n)
    amax = np.abs(w).max(1)
    if fmt == "e4m3":
        byte = np.frexp(amax)[1] - 1 + 127 - 7
    else:
        mant, ex = np.frexp(amax / 6.0)
        byte = np.where(mant > 0.5, ex, ex - 1) + 127
    byte = np.clip(np.where(amax > 0, byte, 1), 1, 254)
    scaled = (w * np.exp2(127.0 - byte)[:, None, :]).reshape(k, n).astype(np.float32)
    by_word = np.ascontiguousarray(scaled.reshape(k // 512, 128, 4, n).transpose(0, 1, 3, 2))
    if fmt == "e4m3":
        words = by_word.astype(ml_dtypes.float8_e4m3fn).view(np.uint8)
    else:
        c = by_word.astype(ml_dtypes.float4_e2m1fn).view(np.uint8) & 0xF
        words = (c[..., 0::2] | (c[..., 1::2] << 4)).reshape(k // 512, 128, 2 * n)
    return np.ascontiguousarray(words), np.ascontiguousarray(byte.astype(np.uint8).reshape(k // 512, 16, n))


def unpack_weight(words, scales, fmt):
    g, _, n = scales.shape
    words = np.ascontiguousarray(words).reshape(g, 128, n, -1)
    if fmt == "e4m3":
        vals = words.view(ml_dtypes.float8_e4m3fn).astype(np.float64)
    else:
        nib = np.empty((g, 128, n, 4), np.uint8)
        nib[..., 0::2] = words & 0xF
        nib[..., 1::2] = words >> 4
        vals = E2M1[nib]
    vals = vals * np.repeat(np.exp2(scales.astype(np.float64) - 127.0), 8, axis=1)[..., None]
    return vals.transpose(0, 1, 3, 2).reshape(g * 512, n)


def gelu(v):
    return 0.5 * v * (1.0 + np.tanh(np.sqrt(2.0 / np.pi) * (v + 0.044715 * v**3)))


K, H, T, S, P = 512, 1024, 4096, 1024, 512

def setup_inputs():
    n = np.random.standard_normal
    s = mx_kscale(K)[:, None]
    u = mx_kscale(H)[:, None]
    tab_words, tab_scales = pack_weight(n((K, T)) * s, "e4m3")
    wb_words, wb_scales = pack_weight(1.2 * n((K, H)) / np.sqrt(K) / s, "e2m1")
    wc_words, wc_scales = pack_weight(n((H, H)) / np.sqrt(H) / u, "e4m3")
    return {
        "tab_words": tab_words, "tab_scales": tab_scales,
        "offs": striped(np.random.permutation(T)[:S]),
        "pos1": striped(np.random.permutation(S)[:P]),
        "wa": (1.2 * n((K, H)) / np.sqrt(K) / s).astype(np.float32),
        "wb_words": wb_words, "wb_scales": wb_scales,
        "gain": (np.exp(0.3 * n(H)) * u[:, 0]).astype(np.float32),
        "wc_words": wc_words, "wc_scales": wc_scales,
        "proof": n((H, P)).astype(np.float32),
        "skip": (np.exp(0.3 * n(H)) / u[:, 0]).astype(np.float32),
        "wgo": np.exp(0.3 * n((128, P))).astype(np.float32),
    }

def reference(tab_words, tab_scales, offs, pos1, wa, wb_words, wb_scales, gain,
              wc_words, wc_scales, proof, skip, wgo):
    v = unpack_weight(tab_words, tab_scales, "e4m3")[:, unstriped(offs)]
    wb = unpack_weight(wb_words, wb_scales, "e2m1")
    wc = unpack_weight(wc_words, wc_scales, "e4m3")
    ink = mxq(f64(wa), 0, "e4m3").T @ v
    grain = wb.T @ v
    h = f64(gain)[:, None] * (np.tanh(ink * grain) + ink)
    x = h[:, unstriped(pos1)]
    y = wc.T @ mxq(x, 0, "e4m3")
    y = np.maximum(y, f64(proof))
    out = f64(skip)[:, None] * h
    out[:, unstriped(pos1)] = np.tile(f64(wgo), (H // 128, 1)) * y
    return out

@@ -1,0 +1,229 @@
+from contextlib import ExitStack
+
+import concourse.mybir as mybir
+
+K, H, T, S, NP = 512, 1024, 4096, 1024, 512
+FLOPS = 2 * (2 * K * H * S + H * H * NP)
+
+F32 = mybir.dt.float32
+BF16 = mybir.dt.bfloat16
+I32 = mybir.dt.int32
+U32 = mybir.dt.uint32
+U16 = mybir.dt.uint16
+U8 = mybir.dt.uint8
+FP8X4 = mybir.dt.float8_e4m3fn_x4
+FP4X4 = mybir.dt.float4_e2m1fn_x4
+ALU = mybir.AluOpType
+ACT = mybir.ActivationFunctionType
+
+P = 128
+PACK = 4
+BANK = 512
+PASSES = H // (P * PACK)
+TILES = PASSES * PACK
+HALVES = S // BANK
+
+
+def tile_list_stone_wear_watch_kernel(
+    tc, tab_words, tab_scales, offs, pos1, wa, wb_words, wb_scales, gain,
+    wc_words, wc_scales, proof, skip, wgo, out,
+):
+    nc = tc.nc
+    with ExitStack() as ctx:
+        keep = ctx.enter_context(tc.tile_pool(name="keep", bufs=1))
+        ring = ctx.enter_context(tc.tile_pool(name="ring", bufs=3))
+        psum = ctx.enter_context(tc.psum_pool(name="psum", bufs=3))
+        psum_y = ctx.enter_context(tc.psum_pool(name="psum_y", bufs=2))
+
+        offs_sb = keep.tile([P, S // 16], U16, name="offs_sb")
+        pos_sb = keep.tile([P, NP // 16], U16, name="pos_sb")
+        tab_w = keep.tile([P, T], U32, name="tab_w", align_bytes=64)
+        tab_s = keep.tile([P, T], U8, name="tab_s", align_bytes=64)
+        w_s_raw = keep.tile([P, H], U8, name="w_s_raw", align_bytes=64)
+        wb_raw = keep.tile([P, 2 * H], U8, name="wb_raw", align_bytes=64)
+        wa_raw = [keep.tile([P, PACK, BANK], F32, name="wa_raw%d" % b) for b in range(PASSES)]
+        wc_raw = [keep.tile([P, H], U32, name="wc_raw%d" % a) for a in range(PASSES)]
+        gain_sb = keep.tile([P, PASSES, PACK], F32, name="gain_sb")
+        skip_sb = keep.tile([P, PASSES, PACK], F32, name="skip_sb")
+        proof_sb = [keep.tile([P, PACK, NP], F32, name="proof_sb%d" % b) for b in range(PASSES)]
+        wgo_sb = keep.tile([P, PACK, NP], F32, name="wgo_sb")
+
+        wc_s_raw = keep.tile([P, H], U8, name="wc_s_raw", align_bytes=64)
+        nc.vector.memset(tab_s[:].bitcast(I32), 0)
+        nc.gpsimd.memset(w_s_raw[:].bitcast(I32), 0)
+        nc.vector.memset(wc_s_raw[:].bitcast(I32), 0)
+
+        wa_v = wa.rearrange("(p j) c -> p j c", j=PACK)
+        nc.sync.dma_start(offs_sb[:], offs)
+        nc.sync.dma_start(pos_sb[:], pos1)
+        nc.scalar.dma_start(gain_sb[:], gain.rearrange("(b p i) -> p b i", p=P, i=PACK))
+        nc.scalar.dma_start(skip_sb[:], skip.rearrange("(b p i) -> p b i", p=P, i=PACK))
+        for q in range(4):
+            nc.scalar.dma_start(tab_s[32 * q : 32 * q + 4, :].bitcast(I32), tab_scales[0, 4 * q : 4 * q + 4, :].bitcast(I32))
+        nc.sync.dma_start(wb_raw[:].bitcast(I32), wb_words[0].bitcast(I32))
+        nc.sync.dma_start(wa_raw[0][:], wa_v[:, :, 0:BANK])
+        nc.sync.dma_start(tab_w[:].bitcast(I32), tab_words[0].rearrange("p t i -> p (t i)").bitcast(I32))
+        for q in range(4):
+            nc.gpsimd.dma_start(w_s_raw[32 * q : 32 * q + 4, :].bitcast(I32), wb_scales[0, 4 * q : 4 * q + 4, :].bitcast(I32))
+        nc.sync.dma_start(wa_raw[1][:], wa_v[:, :, BANK : 2 * BANK])
+        for q in range(4):
+            nc.sync.dma_start(wc_s_raw[32 * q : 32 * q + 8, :].bitcast(I32), wc_scales[:, 4 * q : 4 * q + 4, :].bitcast(I32))
+        for a in range(PASSES):
+            nc.sync.dma_start(wc_raw[a][:].bitcast(I32), wc_words[a].rearrange("p c i -> p (c i)").bitcast(I32))
+        proof_v = proof.rearrange("(b p i) m -> b p i m", p=P, i=PACK)
+        nc.sync.dma_start(proof_sb[0][:], proof_v[0])
+        wgo_v = wgo.rearrange("(q i) m -> q i m", i=PACK)
+        for q in range(4):
+            nc.sync.dma_start(wgo_sb[32 * q : 32 * q + 32], wgo_v)
+        nc.sync.dma_start(proof_sb[1][:], proof_v[1])
+
+        v_s = keep.tile([P, S], U8, name="v_s", align_bytes=64)
+        nc.vector.tensor_copy(v_s[:], tab_s[:].indirect(offs_sb[:]))
+
+        wa_q, wa_s = [], []
+
+        def quantise_wa(b):
+            grouped = keep.tile([P, PACK * P * PACK], BF16, name="wa_grouped%d" % b, align_bytes=64)
+            nc.scalar.copy(
+                grouped[:].rearrange("p (i m j) -> p m i j", i=PACK, j=PACK),
+                wa_raw[b][:].rearrange("p j (m i) -> p m i j", i=PACK),
+            )
+            codes = keep.tile([P, BANK], U32, name="wa_q%d" % b, align_bytes=64)
+            scales = keep.tile([P, BANK], U8, name="wa_s%d" % b, align_bytes=64)
+            nc.vector.quantize_mx(out=codes[:].bitcast(FP8X4), scales=scales[:], in_=grouped[:])
+            wa_q.append(codes)
+            wa_s.append(scales)
+
+        quantise_wa(0)
+
+        wb_q = keep.tile([P, 2 * H], U8, name="wb_q", align_bytes=64)
+        nc.scalar.copy(
+            wb_q[:].bitcast(U16).rearrange("p (b i m) -> p b i m", b=PASSES, i=PACK),
+            wb_raw[:].bitcast(U16).rearrange("p (b m i) -> p b i m", b=PASSES, i=PACK),
+        )
+        w_s = keep.tile([P, H], U8, name="w_s", align_bytes=64)
+        nc.vector.tensor_copy(
+            w_s[:].rearrange("p (b i m) -> p b i m", b=PASSES, i=PACK),
+            w_s_raw[:].rearrange("p (b m i) -> p b i m", b=PASSES, i=PACK),
+        )
+
+        v_q = []
+        for half in range(HALVES):
+            words = keep.tile([P, BANK], U32, name="v_q%d" % half, align_bytes=64)
+            nc.vector.tensor_copy(words[:], tab_w[:].indirect(offs_sb[:, half * 32 : (half + 1) * 32]))
+            v_q.append(words)
+
+        u = [keep.tile([P, S], F32, name="u%d" % n) for n in range(TILES)]
+        x_rows = [keep.tile([P, PACK, NP], BF16, name="x_rows%d" % b) for b in range(PASSES)]
+        x_q, x_s, bent = [], [], {}
+
+        def products(step):
+            n, half = divmod(step, HALVES)
+            b, i = divmod(n, PACK)
+            cols = slice(half * BANK, (half + 1) * BANK)
+            ink = psum.tile([P, BANK], F32, name="ink")
+            grain = psum.tile([P, BANK], F32, name="grain")
+            nc.tensor.matmul_mx(
+                out=ink[:], lhsT=wa_q[b][:, i * P : (i + 1) * P].bitcast(FP8X4), lhsT_scale=wa_s[b][:, i * P : (i + 1) * P],
+                rhs=v_q[half][:].bitcast(FP8X4), rhs_scale=v_s[:, cols], start=True, stop=True,
+            )
+            nc.tensor.matmul_mx(
+                out=grain[:], lhsT=wb_q[:, 2 * n * P : 2 * (n + 1) * P].bitcast(FP4X4), lhsT_scale=w_s[:, n * P : (n + 1) * P],
+                rhs=v_q[half][:].bitcast(FP8X4), rhs_scale=v_s[:, cols], start=True, stop=True,
+            )
+            nc.scalar.copy(u[n][:, cols], ink[:])
+            product = ring.tile([P, BANK], F32, name="product")
+            nc.vector.tensor_tensor(product[:], grain[:], u[n][:, cols], ALU.mult)
+            bent[step] = product
+
+        def bend(step):
+            nc.scalar.activation(bent[step][:], bent[step][:], ACT.Tanh)
+
+        def add_ink(step):
+            n, half = divmod(step, HALVES)
+            cols = slice(half * BANK, (half + 1) * BANK)
+            nc.vector.tensor_tensor(u[n][:, cols], u[n][:, cols], bent[step][:], ALU.add)
+
+        def pick(n):
+            b, i = divmod(n, PACK)
+            picked = ring.tile([P, NP], F32, name="picked")
+            nc.vector.tensor_copy(picked[:], u[n][:].indirect(pos_sb[:]))
+            nc.scalar.activation(x_rows[b][:, i, :], picked[:], ACT.Copy, scale=gain_sb[:, b, i : i + 1])
+
+        def quantise_x(b):
+            woven = keep.tile([P, NP * PACK], BF16, name="x_woven%d" % b, align_bytes=64)
+            dst = woven[:].rearrange("p (c e i) -> p c i e", e=4, i=PACK)
+            src = x_rows[b][:].rearrange("p i (c e) -> p c i e", e=4)
+            if b == 0:
+                nc.scalar.copy(dst, src)
+            else:
+                nc.vector.tensor_copy(dst, src)
+            codes = keep.tile([P, NP], U32, name="x_q%d" % b, align_bytes=64)
+            scales = keep.tile([P, NP], U8, name="x_s%d" % b, align_bytes=64)
+            nc.vector.quantize_mx(out=codes[:].bitcast(FP8X4), scales=scales[:], in_=woven[:])
+            x_q.append(codes)
+            x_s.append(scales)
+
+        wc_s = keep.tile([P, H], U8, name="wc_s", align_bytes=64)
+        steps = TILES * HALVES
+        for step in range(steps + 3):
+            if step < steps:
+                products(step)
+            if 1 <= step <= steps:
+                bend(step - 1)
+            if 2 <= step <= steps + 1:
+                add_ink(step - 2)
+            if step >= 4 and step % HALVES == 0:
+                pick((step - 4) // HALVES)
+            if step == 2:
+                quantise_wa(1)
+            if step == 8:
+                nc.vector.tensor_copy(
+                    wc_s[:].rearrange("p (b i m) -> p b i m", b=PASSES, i=PACK),
+                    wc_s_raw[:].rearrange("p (b m i) -> p b i m", b=PASSES, i=PACK),
+                )
+            if step == 12:
+                quantise_x(0)
+        quantise_x(1)
+
+        wc_q = {}
+
+        def deal_wc(b):
+            for a in range(PASSES):
+                dealt = keep.tile([P, BANK], U32, name="wc_q%d_%d" % (a, b), align_bytes=64)
+                nc.scalar.copy(
+                    dealt[:].rearrange("p (i m) -> p m i", i=PACK),
+                    wc_raw[a][:, b * BANK : (b + 1) * BANK].rearrange("p (m i) -> p m i", i=PACK),
+                )
+                wc_q[a, b] = dealt
+
+        out_v = out.rearrange("(b p i) j -> b i p j", p=P, i=PACK)
+        larger, page = {}, {}
+
+        def second_stage(n):
+            b, i = divmod(n, PACK)
+            if i == 0:
+                deal_wc(b)
+            page[n] = ring.tile([P, S], F32, name="page")
+            nc.scalar.activation(page[n][:], u[n][:], ACT.Copy, scale=gain_sb[:, b, i : i + 1])
+            nc.scalar.activation(page[n][:], page[n][:], ACT.Copy, scale=skip_sb[:, b, i : i + 1])
+            y = psum_y.tile([P, NP], F32, name="y")
+            for a in range(PASSES):
+                nc.tensor.matmul_mx(
+                    out=y[:], lhsT=wc_q[a, b][:, i * P : (i + 1) * P].bitcast(FP8X4),
+                    lhsT_scale=wc_s[4 * a :, n * P : (n + 1) * P],
+                    rhs=x_q[a][:].bitcast(FP8X4), rhs_scale=x_s[a][:], start=(a == 0), stop=(a == PASSES - 1),
+                )
+            larger[n] = ring.tile([P, NP], F32, name="larger")
+            nc.vector.tensor_tensor(larger[n][:], y[:], proof_sb[b][:, i, :], ALU.max)
+
+        def put(n):
+            b, i = divmod(n, PACK)
+            nc.vector.tensor_tensor(page[n][:].indirect(pos_sb[:]), larger[n][:], wgo_sb[:, i, :], ALU.mult)
+            nc.sync.dma_start(out_v[b, i], page[n][:])
+
+        for n in range(TILES + 1):
+            if n < TILES:
+                second_stage(n)
+            if n >= 1:
+                put(n - 1)

@@ -22,6 +22,12 @@ BANK = 512
 PASSES = H // (P * PACK)
 TILES = PASSES * PACK
 HALVES = S // BANK
+GP_TILES = (0, 2, 4)
+V_STEPS = (3, 7, 11, 15)
+LAG = 2
+WA1_STEP = 1
+WC_TAGS = ("product9", "product7")
+PAGE_TAGS = ("slot2", "x_rows1", "x_woven1_1")
 
 
 def tile_list_stone_wear_watch_kernel(
@@ -32,8 +38,7 @@ def tile_list_stone_wear_watch_kernel(
     with ExitStack() as ctx:
         keep = ctx.enter_context(tc.tile_pool(name="keep", bufs=1))
         ring = ctx.enter_context(tc.tile_pool(name="ring", bufs=3))
-        psum = ctx.enter_context(tc.psum_pool(name="psum", bufs=3))
-        psum_y = ctx.enter_context(tc.psum_pool(name="psum_y", bufs=2))
+        psum = ctx.enter_context(tc.psum_pool(name="psum", bufs=4))
 
         offs_sb = keep.tile([P, S // 16], U16, name="offs_sb")
         pos_sb = keep.tile([P, NP // 16], U16, name="pos_sb")
@@ -42,7 +47,7 @@ def tile_list_stone_wear_watch_kernel(
         w_s_raw = keep.tile([P, H], U8, name="w_s_raw", align_bytes=64)
         wb_raw = keep.tile([P, 2 * H], U8, name="wb_raw", align_bytes=64)
         wa_raw = [keep.tile([P, PACK, BANK], F32, name="wa_raw%d" % b) for b in range(PASSES)]
-        wc_raw = [keep.tile([P, H], U32, name="wc_raw%d" % a) for a in range(PASSES)]
+        wc_raw = keep.tile([P, PASSES, H], U32, name="wc_raw")
         gain_sb = keep.tile([P, PASSES, PACK], F32, name="gain_sb")
         skip_sb = keep.tile([P, PASSES, PACK], F32, name="skip_sb")
         proof_sb = [keep.tile([P, PACK, NP], F32, name="proof_sb%d" % b) for b in range(PASSES)]
@@ -51,25 +56,24 @@ def tile_list_stone_wear_watch_kernel(
         wc_s_raw = keep.tile([P, H], U8, name="wc_s_raw", align_bytes=64)
         nc.vector.memset(tab_s[:].bitcast(I32), 0)
         nc.gpsimd.memset(w_s_raw[:].bitcast(I32), 0)
-        nc.vector.memset(wc_s_raw[:].bitcast(I32), 0)
+        nc.gpsimd.memset(wc_s_raw[:].bitcast(I32), 0)
 
         wa_v = wa.rearrange("(p j) c -> p j c", j=PACK)
         nc.sync.dma_start(offs_sb[:], offs)
-        nc.sync.dma_start(pos_sb[:], pos1)
-        nc.scalar.dma_start(gain_sb[:], gain.rearrange("(b p i) -> p b i", p=P, i=PACK))
-        nc.scalar.dma_start(skip_sb[:], skip.rearrange("(b p i) -> p b i", p=P, i=PACK))
-        for q in range(4):
-            nc.scalar.dma_start(tab_s[32 * q : 32 * q + 4, :].bitcast(I32), tab_scales[0, 4 * q : 4 * q + 4, :].bitcast(I32))
         nc.sync.dma_start(wb_raw[:].bitcast(I32), wb_words[0].bitcast(I32))
         nc.sync.dma_start(wa_raw[0][:], wa_v[:, :, 0:BANK])
+        for q in range(4):
+            nc.sync.dma_start(tab_s[32 * q : 32 * q + 4, :].bitcast(I32), tab_scales[0, 4 * q : 4 * q + 4, :].bitcast(I32))
         nc.sync.dma_start(tab_w[:].bitcast(I32), tab_words[0].rearrange("p t i -> p (t i)").bitcast(I32))
         for q in range(4):
-            nc.gpsimd.dma_start(w_s_raw[32 * q : 32 * q + 4, :].bitcast(I32), wb_scales[0, 4 * q : 4 * q + 4, :].bitcast(I32))
+            nc.scalar.dma_start(w_s_raw[32 * q : 32 * q + 4, :].bitcast(I32), wb_scales[0, 4 * q : 4 * q + 4, :].bitcast(I32))
         nc.sync.dma_start(wa_raw[1][:], wa_v[:, :, BANK : 2 * BANK])
+        nc.sync.dma_start(pos_sb[:], pos1)
+        nc.sync.dma_start(gain_sb[:], gain.rearrange("(b p i) -> p b i", p=P, i=PACK))
         for q in range(4):
             nc.sync.dma_start(wc_s_raw[32 * q : 32 * q + 8, :].bitcast(I32), wc_scales[:, 4 * q : 4 * q + 4, :].bitcast(I32))
-        for a in range(PASSES):
-            nc.sync.dma_start(wc_raw[a][:].bitcast(I32), wc_words[a].rearrange("p c i -> p (c i)").bitcast(I32))
+        nc.sync.dma_start(skip_sb[:], skip.rearrange("(b p i) -> p b i", p=P, i=PACK))
+        nc.sync.dma_start(wc_raw[:].bitcast(I32), wc_words.rearrange("a p c i -> p a (c i)").bitcast(I32))
         proof_v = proof.rearrange("(b p i) m -> b p i m", p=P, i=PACK)
         nc.sync.dma_start(proof_sb[0][:], proof_v[0])
         wgo_v = wgo.rearrange("(q i) m -> q i m", i=PACK)
@@ -84,10 +88,12 @@ def tile_list_stone_wear_watch_kernel(
 
         def quantise_wa(b):
             grouped = keep.tile([P, PACK * P * PACK], BF16, name="wa_grouped%d" % b, align_bytes=64)
-            nc.scalar.copy(
-                grouped[:].rearrange("p (i m j) -> p m i j", i=PACK, j=PACK),
-                wa_raw[b][:].rearrange("p j (m i) -> p m i j", i=PACK),
-            )
+            dst = grouped[:].rearrange("p (i m j) -> p m i j", i=PACK, j=PACK)
+            src = wa_raw[b][:].rearrange("p j (m i) -> p m i j", i=PACK)
+            if b == 0:
+                nc.scalar.activation(dst, src, ACT.Copy)
+            else:
+                nc.vector.tensor_copy(dst, src)
             codes = keep.tile([P, BANK], U32, name="wa_q%d" % b, align_bytes=64)
             scales = keep.tile([P, BANK], U8, name="wa_s%d" % b, align_bytes=64)
             nc.vector.quantize_mx(out=codes[:].bitcast(FP8X4), scales=scales[:], in_=grouped[:])
@@ -102,10 +108,11 @@ def tile_list_stone_wear_watch_kernel(
             wb_raw[:].bitcast(U16).rearrange("p (b m i) -> p b i m", b=PASSES, i=PACK),
         )
         w_s = keep.tile([P, H], U8, name="w_s", align_bytes=64)
-        nc.vector.tensor_copy(
-            w_s[:].rearrange("p (b i m) -> p b i m", b=PASSES, i=PACK),
-            w_s_raw[:].rearrange("p (b m i) -> p b i m", b=PASSES, i=PACK),
-        )
+        for b in range(PASSES):
+            nc.gpsimd.tensor_copy(
+                w_s[:, b * BANK : (b + 1) * BANK].rearrange("p (i m) -> p i m", i=PACK),
+                w_s_raw[:, b * BANK : (b + 1) * BANK].rearrange("p (m i) -> p i m", i=PACK),
+            )
 
         v_q = []
         for half in range(HALVES):
@@ -114,8 +121,8 @@ def tile_list_stone_wear_watch_kernel(
             v_q.append(words)
 
         u = [keep.tile([P, S], F32, name="u%d" % n) for n in range(TILES)]
-        x_rows = [keep.tile([P, PACK, NP], BF16, name="x_rows%d" % b) for b in range(PASSES)]
-        x_q, x_s, bent = [], [], {}
+        x_rows = [keep.tile([P, PACK, NP], BF16, name="x_rows", tag="x_rows%d" % b, align_bytes=64) for b in range(PASSES)]
+        x_q, x_s, bent, products_sb, inks = [], [], {}, {}, {}
 
         def products(step):
             n, half = divmod(step, HALVES)
@@ -132,85 +139,90 @@ def tile_list_stone_wear_watch_kernel(
                 rhs=v_q[half][:].bitcast(FP8X4), rhs_scale=v_s[:, cols], start=True, stop=True,
             )
             nc.scalar.copy(u[n][:, cols], ink[:])
-            product = ring.tile([P, BANK], F32, name="product")
+            product = keep.tile([P, BANK], F32, name="product", tag="product%d" % step, align_bytes=64)
             nc.vector.tensor_tensor(product[:], grain[:], u[n][:, cols], ALU.mult)
-            bent[step] = product
+            products_sb[step] = product
+            inks[step] = ink
 
         def bend(step):
-            nc.scalar.activation(bent[step][:], bent[step][:], ACT.Tanh)
+            bent[step] = keep.tile([P, BANK], F32, name="bent", tag="slot%d" % (step % 3), align_bytes=64)
+            nc.scalar.activation(bent[step][:], products_sb[step][:], ACT.Tanh)
 
         def add_ink(step):
             n, half = divmod(step, HALVES)
             cols = slice(half * BANK, (half + 1) * BANK)
-            nc.vector.tensor_tensor(u[n][:, cols], u[n][:, cols], bent[step][:], ALU.add)
+            if step in V_STEPS:
+                nc.vector.tensor_tensor(u[n][:, cols], inks[step][:], bent[step][:], ALU.add)
+            else:
+                nc.gpsimd.tensor_tensor(u[n][:, cols], u[n][:, cols], bent[step][:], ALU.add)
 
         def pick(n):
             b, i = divmod(n, PACK)
-            picked = ring.tile([P, NP], F32, name="picked")
+            picked = keep.tile([P, NP], F32, name="picked", tag="product%d" % (2 * n + LAG), align_bytes=64)
             nc.vector.tensor_copy(picked[:], u[n][:].indirect(pos_sb[:]))
-            nc.scalar.activation(x_rows[b][:, i, :], picked[:], ACT.Copy, scale=gain_sb[:, b, i : i + 1])
+            if n in GP_TILES:
+                nc.gpsimd.tensor_scalar(x_rows[b][:, i, :], picked[:], gain_sb[:, b, i : i + 1], 0.0, ALU.mult, ALU.add)
+            else:
+                nc.scalar.activation(x_rows[b][:, i, :], picked[:], ACT.Copy, scale=gain_sb[:, b, i : i + 1])
 
         def quantise_x(b):
-            woven = keep.tile([P, NP * PACK], BF16, name="x_woven%d" % b, align_bytes=64)
-            dst = woven[:].rearrange("p (c e i) -> p c i e", e=4, i=PACK)
-            src = x_rows[b][:].rearrange("p i (c e) -> p c i e", e=4)
-            if b == 0:
-                nc.scalar.copy(dst, src)
-            else:
-                nc.vector.tensor_copy(dst, src)
             codes = keep.tile([P, NP], U32, name="x_q%d" % b, align_bytes=64)
             scales = keep.tile([P, NP], U8, name="x_s%d" % b, align_bytes=64)
-            nc.vector.quantize_mx(out=codes[:].bitcast(FP8X4), scales=scales[:], in_=woven[:])
+            parts = 1 if b == 0 else 2
+            width = NP // parts
+            for part in range(parts):
+                cols = slice(part * width, (part + 1) * width)
+                woven = keep.tile([P, width * PACK], BF16, name="x_woven", tag=("product15" if b == 0 else "x_woven1_%d" % part), align_bytes=64)
+                dst = woven[:].rearrange("p (c e i) -> p c i e", e=4, i=PACK)
+                src = x_rows[b][:, :, cols].rearrange("p i (c e) -> p c i e", e=4)
+                if b == 0 and False:
+                    nc.gpsimd.tensor_copy(dst, src)
+                elif b == 0 or part == 1:
+                    nc.scalar.copy(dst, src)
+                else:
+                    nc.vector.tensor_copy(dst, src)
+                nc.vector.quantize_mx(out=codes[:, cols].bitcast(FP8X4), scales=scales[:, cols], in_=woven[:])
             x_q.append(codes)
             x_s.append(scales)
 
-        wc_s = keep.tile([P, H], U8, name="wc_s", align_bytes=64)
         steps = TILES * HALVES
-        for step in range(steps + 3):
+        for step in range(steps + 6):
+            if step == WA1_STEP:
+                quantise_wa(1)
             if step < steps:
                 products(step)
-            if 1 <= step <= steps:
-                bend(step - 1)
-            if 2 <= step <= steps + 1:
-                add_ink(step - 2)
-            if step >= 4 and step % HALVES == 0:
-                pick((step - 4) // HALVES)
-            if step == 2:
-                quantise_wa(1)
-            if step == 8:
-                nc.vector.tensor_copy(
-                    wc_s[:].rearrange("p (b i m) -> p b i m", b=PASSES, i=PACK),
-                    wc_s_raw[:].rearrange("p (b m i) -> p b i m", b=PASSES, i=PACK),
-                )
-            if step == 12:
+            if 2 <= step < steps + 2:
+                bend(step - 2)
+            if 3 <= step < steps + 3:
+                add_ink(step - 3)
+            if step >= 7 and step % HALVES == 1:
+                pick((step - 7) // HALVES)
+            if step == 15 + 2:
                 quantise_x(0)
         quantise_x(1)
 
-        wc_q = {}
-
-        def deal_wc(b):
-            for a in range(PASSES):
-                dealt = keep.tile([P, BANK], U32, name="wc_q%d_%d" % (a, b), align_bytes=64)
-                nc.scalar.copy(
-                    dealt[:].rearrange("p (i m) -> p m i", i=PACK),
-                    wc_raw[a][:, b * BANK : (b + 1) * BANK].rearrange("p (m i) -> p m i", i=PACK),
-                )
-                wc_q[a, b] = dealt
-
+        wc_s = keep.tile([P, H], U8, name="wc_s", tag="slot1", align_bytes=64)
+        nc.gpsimd.tensor_copy(
+            wc_s[:].rearrange("p (b i m) -> p b i m", b=PASSES, i=PACK),
+            wc_s_raw[:].rearrange("p (b m i) -> p b i m", b=PASSES, i=PACK),
+        )
         out_v = out.rearrange("(b p i) j -> b i p j", p=P, i=PACK)
         larger, page = {}, {}
 
         def second_stage(n):
             b, i = divmod(n, PACK)
-            if i == 0:
-                deal_wc(b)
-            page[n] = ring.tile([P, S], F32, name="page")
-            nc.scalar.activation(page[n][:], u[n][:], ACT.Copy, scale=gain_sb[:, b, i : i + 1])
-            nc.scalar.activation(page[n][:], page[n][:], ACT.Copy, scale=skip_sb[:, b, i : i + 1])
-            y = psum_y.tile([P, NP], F32, name="y")
+            wc_q = keep.tile([P, PASSES, P], U32, name="wc_q", tag=WC_TAGS[n % 2], align_bytes=64)
+            nc.scalar.copy(wc_q[:], wc_raw[:, :, b * BANK + i : (b + 1) * BANK : PACK])
+            page[n] = keep.tile([P, S], F32, name="page", tag=PAGE_TAGS[n % 3], align_bytes=64)
+            if n == 0:
+                nc.gpsimd.tensor_scalar(page[n][:], u[n][:], gain_sb[:, b, i : i + 1], skip_sb[:, b, i : i + 1], ALU.mult, ALU.mult)
+            else:
+                nc.scalar.activation(page[n][:], u[n][:], ACT.Copy, scale=gain_sb[:, b, i : i + 1])
+                nc.scalar.activation(page[n][:], page[n][:], ACT.Copy, scale=skip_sb[:, b, i : i + 1])
+            y = psum.tile([P, NP], F32, name="y", tag="grain")
             for a in range(PASSES):
                 nc.tensor.matmul_mx(
-                    out=y[:], lhsT=wc_q[a, b][:, i * P : (i + 1) * P].bitcast(FP8X4),
+                    out=y[:], lhsT=wc_q[:, a, :].bitcast(FP8X4),
                     lhsT_scale=wc_s[4 * a :, n * P : (n + 1) * P],
                     rhs=x_q[a][:].bitcast(FP8X4), rhs_scale=x_s[a][:], start=(a == 0), stop=(a == PASSES - 1),
                 )

@@ -2,8 +2,8 @@ from contextlib import ExitStack
 
 import concourse.mybir as mybir
 
-K, H, T, S, NP = 512, 1024, 4096, 1024, 512
-FLOPS = 2 * (2 * K * H * S + H * H * NP)
+K, H, T, S, PICKED = 512, 1024, 4096, 1024, 512
+FLOPS = 2 * (2 * K * H * S + H * H * PICKED)
 
 F32 = mybir.dt.float32
 BF16 = mybir.dt.bfloat16
@@ -18,16 +18,24 @@ ACT = mybir.ActivationFunctionType
 
 P = 128
 PACK = 4
+QUADRANTS = 4
+LIST_ROWS = 16
 BANK = 512
-PASSES = H // (P * PACK)
+PASSES = H // BANK
 TILES = PASSES * PACK
-HALVES = S // BANK
-GP_TILES = (0, 2, 4)
-V_STEPS = (3, 7, 11, 15)
-LAG = 2
-WA1_STEP = 1
-WC_TAGS = ("product9", "product7")
-PAGE_TAGS = ("slot2", "x_rows1", "x_woven1_1")
+TANH_BUFFERS = 3
+TANH_LAG, SUM_LAG = 2, 3
+PICK_LAG = 6
+WC_PIECE = 9
+
+
+def offsets(list_tile, cols):
+    return list_tile[:, cols.start // LIST_ROWS : cols.stop // LIST_ROWS]
+
+
+def halves(cols):
+    middle = (cols.start + cols.stop) // 2
+    return [slice(cols.start, middle), slice(middle, cols.stop)]
 
 
 def tile_list_stone_wear_watch_kernel(
@@ -40,62 +48,71 @@ def tile_list_stone_wear_watch_kernel(
         ring = ctx.enter_context(tc.tile_pool(name="ring", bufs=3))
         psum = ctx.enter_context(tc.psum_pool(name="psum", bufs=4))
 
-        offs_sb = keep.tile([P, S // 16], U16, name="offs_sb")
-        pos_sb = keep.tile([P, NP // 16], U16, name="pos_sb")
+        offs_sb = keep.tile([P, S // LIST_ROWS], U16, name="offs_sb")
+        pos_sb = keep.tile([P, PICKED // LIST_ROWS], U16, name="pos_sb")
         tab_w = keep.tile([P, T], U32, name="tab_w", align_bytes=64)
         tab_s = keep.tile([P, T], U8, name="tab_s", align_bytes=64)
-        w_s_raw = keep.tile([P, H], U8, name="w_s_raw", align_bytes=64)
+        wb_s_raw = keep.tile([P, H], U8, name="wb_s_raw", align_bytes=64)
         wb_raw = keep.tile([P, 2 * H], U8, name="wb_raw", align_bytes=64)
-        wa_raw = [keep.tile([P, PACK, BANK], F32, name="wa_raw%d" % b) for b in range(PASSES)]
+        first_pass, second_pass = halves(slice(0, H))
+        wa_first = [keep.tile([P, PACK, BANK // 2], F32, name="wa_first%d" % h, align_bytes=64) for h in range(2)]
+        wa_second = keep.tile([P, PACK, BANK], F32, name="wa_second")
         wc_raw = keep.tile([P, PASSES, H], U32, name="wc_raw")
         gain_sb = keep.tile([P, PASSES, PACK], F32, name="gain_sb")
         skip_sb = keep.tile([P, PASSES, PACK], F32, name="skip_sb")
-        proof_sb = [keep.tile([P, PACK, NP], F32, name="proof_sb%d" % b) for b in range(PASSES)]
-        wgo_sb = keep.tile([P, PACK, NP], F32, name="wgo_sb")
-
+        proof_sb = [keep.tile([P, PACK, PICKED], F32, name="proof_sb%d" % b) for b in range(PASSES)]
+        wgo_sb = keep.tile([P, PACK, PICKED], F32, name="wgo_sb")
         wc_s_raw = keep.tile([P, H], U8, name="wc_s_raw", align_bytes=64)
+
         nc.vector.memset(tab_s[:].bitcast(I32), 0)
-        nc.gpsimd.memset(w_s_raw[:].bitcast(I32), 0)
+        nc.gpsimd.memset(wb_s_raw[:].bitcast(I32), 0)
         nc.gpsimd.memset(wc_s_raw[:].bitcast(I32), 0)
 
-        wa_v = wa.rearrange("(p j) c -> p j c", j=PACK)
+        wa_v = wa.rearrange("(p t) c -> p t c", t=PACK)
         nc.sync.dma_start(offs_sb[:], offs)
-        nc.sync.dma_start(wb_raw[:].bitcast(I32), wb_words[0].bitcast(I32))
-        nc.sync.dma_start(wa_raw[0][:], wa_v[:, :, 0:BANK])
-        for q in range(4):
+        nc.sync.dma_start(wa_first[0][:], wa_v[:, :, halves(first_pass)[0]])
+        for q in range(QUADRANTS):
             nc.sync.dma_start(tab_s[32 * q : 32 * q + 4, :].bitcast(I32), tab_scales[0, 4 * q : 4 * q + 4, :].bitcast(I32))
+        nc.sync.dma_start(wa_first[1][:], wa_v[:, :, halves(first_pass)[1]])
+        nc.sync.dma_start(wb_raw[:].bitcast(I32), wb_words[0].bitcast(I32))
+        for q in range(QUADRANTS):
+            nc.sync.dma_start(wb_s_raw[32 * q : 32 * q + 4, :].bitcast(I32), wb_scales[0, 4 * q : 4 * q + 4, :].bitcast(I32))
         nc.sync.dma_start(tab_w[:].bitcast(I32), tab_words[0].rearrange("p t i -> p (t i)").bitcast(I32))
-        for q in range(4):
-            nc.scalar.dma_start(w_s_raw[32 * q : 32 * q + 4, :].bitcast(I32), wb_scales[0, 4 * q : 4 * q + 4, :].bitcast(I32))
-        nc.sync.dma_start(wa_raw[1][:], wa_v[:, :, BANK : 2 * BANK])
+        nc.sync.dma_start(wa_second[:], wa_v[:, :, second_pass])
         nc.sync.dma_start(pos_sb[:], pos1)
         nc.sync.dma_start(gain_sb[:], gain.rearrange("(b p i) -> p b i", p=P, i=PACK))
-        for q in range(4):
+        for q in range(QUADRANTS):
             nc.sync.dma_start(wc_s_raw[32 * q : 32 * q + 8, :].bitcast(I32), wc_scales[:, 4 * q : 4 * q + 4, :].bitcast(I32))
         nc.sync.dma_start(skip_sb[:], skip.rearrange("(b p i) -> p b i", p=P, i=PACK))
         nc.sync.dma_start(wc_raw[:].bitcast(I32), wc_words.rearrange("a p c i -> p a (c i)").bitcast(I32))
         proof_v = proof.rearrange("(b p i) m -> b p i m", p=P, i=PACK)
         nc.sync.dma_start(proof_sb[0][:], proof_v[0])
         wgo_v = wgo.rearrange("(q i) m -> q i m", i=PACK)
-        for q in range(4):
+        for q in range(QUADRANTS):
             nc.sync.dma_start(wgo_sb[32 * q : 32 * q + 32], wgo_v)
         nc.sync.dma_start(proof_sb[1][:], proof_v[1])
 
         v_s = keep.tile([P, S], U8, name="v_s", align_bytes=64)
         nc.vector.tensor_copy(v_s[:], tab_s[:].indirect(offs_sb[:]))
 
+        left, right = halves(slice(0, S))
+        v_q = [keep.tile([P, BANK], U32, name="v_q%d" % bank, align_bytes=64) for bank in range(S // BANK)]
+        for cols in halves(left):
+            nc.vector.tensor_copy(v_q[0][:, cols], tab_w[:].indirect(offsets(offs_sb, cols)))
+        nc.vector.tensor_copy(v_q[1][:], tab_w[:].indirect(offsets(offs_sb, right)))
+
         wa_q, wa_s = [], []
 
         def quantise_wa(b):
             grouped = keep.tile([P, PACK * P * PACK], BF16, name="wa_grouped%d" % b, align_bytes=64)
-            dst = grouped[:].rearrange("p (i m j) -> p m i j", i=PACK, j=PACK)
-            src = wa_raw[b][:].rearrange("p j (m i) -> p m i j", i=PACK)
-            if b == 0:
-                nc.scalar.activation(dst, src, ACT.Copy)
-            else:
-                nc.vector.tensor_copy(dst, src)
+            dst = grouped[:].rearrange("p (i m t) -> p m i t", i=PACK, t=PACK)
             codes = keep.tile([P, BANK], U32, name="wa_q%d" % b, align_bytes=64)
             scales = keep.tile([P, BANK], U8, name="wa_s%d" % b, align_bytes=64)
+            if b == 0:
+                for raw, places in zip(wa_first, halves(slice(0, P))):
+                    nc.scalar.activation(dst[:, places], raw[:].rearrange("p t (m i) -> p m i t", i=PACK), ACT.Copy)
+            else:
+                nc.vector.tensor_copy(dst, wa_second[:].rearrange("p t (m i) -> p m i t", i=PACK))
             nc.vector.quantize_mx(out=codes[:].bitcast(FP8X4), scales=scales[:], in_=grouped[:])
             wa_q.append(codes)
             wa_s.append(scales)
@@ -103,139 +120,145 @@ def tile_list_stone_wear_watch_kernel(
         quantise_wa(0)
 
         wb_q = keep.tile([P, 2 * H], U8, name="wb_q", align_bytes=64)
-        nc.scalar.copy(
-            wb_q[:].bitcast(U16).rearrange("p (b i m) -> p b i m", b=PASSES, i=PACK),
-            wb_raw[:].bitcast(U16).rearrange("p (b m i) -> p b i m", b=PASSES, i=PACK),
-        )
-        w_s = keep.tile([P, H], U8, name="w_s", align_bytes=64)
         for b in range(PASSES):
-            nc.gpsimd.tensor_copy(
-                w_s[:, b * BANK : (b + 1) * BANK].rearrange("p (i m) -> p i m", i=PACK),
-                w_s_raw[:, b * BANK : (b + 1) * BANK].rearrange("p (m i) -> p i m", i=PACK),
+            nc.scalar.copy(
+                wb_q[:, b * H : (b + 1) * H].bitcast(U16).rearrange("p (i m) -> p i m", i=PACK),
+                wb_raw[:, b * H : (b + 1) * H].bitcast(U16).rearrange("p (m i) -> p i m", i=PACK),
+            )
+        wb_s = [keep.tile([P, BANK], U8, name="wb_s%d" % b, align_bytes=64) for b in range(PASSES)]
+        for b in range(PASSES):
+            nc.vector.tensor_copy(
+                wb_s[b][:].rearrange("p (i m) -> p i m", i=PACK),
+                wb_s_raw[:, b * BANK : (b + 1) * BANK].rearrange("p (m i) -> p i m", i=PACK),
             )
 
-        v_q = []
-        for half in range(HALVES):
-            words = keep.tile([P, BANK], U32, name="v_q%d" % half, align_bytes=64)
-            nc.vector.tensor_copy(words[:], tab_w[:].indirect(offs_sb[:, half * 32 : (half + 1) * 32]))
-            v_q.append(words)
+        quantise_wa(1)
 
         u = [keep.tile([P, S], F32, name="u%d" % n) for n in range(TILES)]
-        x_rows = [keep.tile([P, PACK, NP], BF16, name="x_rows", tag="x_rows%d" % b, align_bytes=64) for b in range(PASSES)]
-        x_q, x_s, bent, products_sb, inks = [], [], {}, {}, {}
+        x_rows = [keep.tile([P, PACK, PICKED], BF16, name="x_rows", tag="x_rows%d" % b, align_bytes=64) for b in range(PASSES)]
+        wc_s = keep.tile([P, H], U8, name="wc_s", align_bytes=64)
 
-        def products(step):
-            n, half = divmod(step, HALVES)
+        pieces = [(0, cols) for cols in halves(left)] + [(1, left), (0, right), (1, right)]
+        pieces.extend((n, cols) for n in range(2, TILES) for cols in (left, right))
+        last_piece = {n: k for k, (n, cols) in enumerate(pieces)}
+        ink, product, bent, x_q, x_s, wc_q, page = {}, {}, {}, [], [], {}, {}
+
+        def products(k):
+            n, cols = pieces[k]
             b, i = divmod(n, PACK)
-            cols = slice(half * BANK, (half + 1) * BANK)
-            ink = psum.tile([P, BANK], F32, name="ink")
-            grain = psum.tile([P, BANK], F32, name="grain")
+            width = cols.stop - cols.start
+            bank = cols.start // BANK
+            moving = v_q[bank][:, cols.start - bank * BANK : cols.stop - bank * BANK].bitcast(FP8X4)
+            place = slice(i * P, (i + 1) * P)
+            ink[k] = psum.tile([P, width], F32, name="ink")
+            grain = psum.tile([P, width], F32, name="grain")
             nc.tensor.matmul_mx(
-                out=ink[:], lhsT=wa_q[b][:, i * P : (i + 1) * P].bitcast(FP8X4), lhsT_scale=wa_s[b][:, i * P : (i + 1) * P],
-                rhs=v_q[half][:].bitcast(FP8X4), rhs_scale=v_s[:, cols], start=True, stop=True,
+                out=ink[k][:], lhsT=wa_q[b][:, place].bitcast(FP8X4), lhsT_scale=wa_s[b][:, place],
+                rhs=moving, rhs_scale=v_s[:, cols], start=True, stop=True,
             )
             nc.tensor.matmul_mx(
-                out=grain[:], lhsT=wb_q[:, 2 * n * P : 2 * (n + 1) * P].bitcast(FP4X4), lhsT_scale=w_s[:, n * P : (n + 1) * P],
-                rhs=v_q[half][:].bitcast(FP8X4), rhs_scale=v_s[:, cols], start=True, stop=True,
+                out=grain[:], lhsT=wb_q[:, 2 * n * P : 2 * (n + 1) * P].bitcast(FP4X4), lhsT_scale=wb_s[b][:, place],
+                rhs=moving, rhs_scale=v_s[:, cols], start=True, stop=True,
             )
-            nc.scalar.copy(u[n][:, cols], ink[:])
-            product = keep.tile([P, BANK], F32, name="product", tag="product%d" % step, align_bytes=64)
-            nc.vector.tensor_tensor(product[:], grain[:], u[n][:, cols], ALU.mult)
-            products_sb[step] = product
-            inks[step] = ink
+            nc.scalar.copy(u[n][:, cols], ink[k][:])
+            product[k] = keep.tile([P, width], F32, name="product", tag="product%d" % k, align_bytes=64)
+            nc.vector.tensor_tensor(product[k][:], grain[:], u[n][:, cols], ALU.mult)
 
-        def bend(step):
-            bent[step] = keep.tile([P, BANK], F32, name="bent", tag="slot%d" % (step % 3), align_bytes=64)
-            nc.scalar.activation(bent[step][:], products_sb[step][:], ACT.Tanh)
+        def bend(k):
+            n, cols = pieces[k]
+            bent[k] = keep.tile([P, cols.stop - cols.start], F32, name="bent", tag="bent%d" % (k % TANH_BUFFERS), align_bytes=64)
+            nc.scalar.activation(bent[k][:], product[k][:], ACT.Tanh)
 
-        def add_ink(step):
-            n, half = divmod(step, HALVES)
-            cols = slice(half * BANK, (half + 1) * BANK)
-            if step in V_STEPS:
-                nc.vector.tensor_tensor(u[n][:, cols], inks[step][:], bent[step][:], ALU.add)
+        def add_ink(k):
+            n, cols = pieces[k]
+            if cols == right and (n % 2 == 0 or n == TILES - 1):
+                nc.vector.tensor_tensor(u[n][:, cols], ink[k][:], bent[k][:], ALU.add)
             else:
-                nc.gpsimd.tensor_tensor(u[n][:, cols], u[n][:, cols], bent[step][:], ALU.add)
+                nc.gpsimd.tensor_tensor(u[n][:, cols], u[n][:, cols], bent[k][:], ALU.add)
 
         def pick(n):
             b, i = divmod(n, PACK)
-            picked = keep.tile([P, NP], F32, name="picked", tag="product%d" % (2 * n + LAG), align_bytes=64)
-            nc.vector.tensor_copy(picked[:], u[n][:].indirect(pos_sb[:]))
-            if n in GP_TILES:
-                nc.gpsimd.tensor_scalar(x_rows[b][:, i, :], picked[:], gain_sb[:, b, i : i + 1], 0.0, ALU.mult, ALU.add)
-            else:
-                nc.scalar.activation(x_rows[b][:, i, :], picked[:], ACT.Copy, scale=gain_sb[:, b, i : i + 1])
+            every = slice(0, PICKED)
+            for part, cols in enumerate(halves(every) if n == TILES - 1 else [every]):
+                picked = keep.tile([P, cols.stop - cols.start], F32, name="picked", tag="product%d" % (2 * n + 3 + part), align_bytes=64)
+                nc.vector.tensor_copy(picked[:], u[n][:].indirect(offsets(pos_sb, cols)))
+                if n % 2 == 1 and n < TILES - 1:
+                    nc.gpsimd.tensor_scalar(x_rows[b][:, i, cols], picked[:], gain_sb[:, b, i : i + 1], 0.0, ALU.mult, ALU.add)
+                else:
+                    nc.scalar.activation(x_rows[b][:, i, cols], picked[:], ACT.Copy, scale=gain_sb[:, b, i : i + 1])
 
         def quantise_x(b):
-            codes = keep.tile([P, NP], U32, name="x_q%d" % b, align_bytes=64)
-            scales = keep.tile([P, NP], U8, name="x_s%d" % b, align_bytes=64)
-            parts = 1 if b == 0 else 2
-            width = NP // parts
-            for part in range(parts):
-                cols = slice(part * width, (part + 1) * width)
-                woven = keep.tile([P, width * PACK], BF16, name="x_woven", tag=("product15" if b == 0 else "x_woven1_%d" % part), align_bytes=64)
+            codes = keep.tile([P, PICKED], U32, name="x_q%d" % b, align_bytes=64)
+            scales = keep.tile([P, PICKED], U8, name="x_s%d" % b, align_bytes=64)
+            for part, cols in enumerate(halves(slice(0, PICKED))):
+                tag = "product%d" % last_piece[TILES - 2 + part] if b == 0 else "x_woven%d" % part
+                woven = keep.tile([P, (cols.stop - cols.start) * PACK], BF16, name="x_woven", tag=tag, align_bytes=64)
                 dst = woven[:].rearrange("p (c e i) -> p c i e", e=4, i=PACK)
                 src = x_rows[b][:, :, cols].rearrange("p i (c e) -> p c i e", e=4)
-                if b == 0 and False:
-                    nc.gpsimd.tensor_copy(dst, src)
-                elif b == 0 or part == 1:
-                    nc.scalar.copy(dst, src)
-                else:
+                if b == PASSES - 1 and part == 0:
                     nc.vector.tensor_copy(dst, src)
+                else:
+                    nc.scalar.copy(dst, src)
                 nc.vector.quantize_mx(out=codes[:, cols].bitcast(FP8X4), scales=scales[:, cols], in_=woven[:])
             x_q.append(codes)
             x_s.append(scales)
 
-        steps = TILES * HALVES
-        for step in range(steps + 6):
-            if step == WA1_STEP:
-                quantise_wa(1)
-            if step < steps:
-                products(step)
-            if 2 <= step < steps + 2:
-                bend(step - 2)
-            if 3 <= step < steps + 3:
-                add_ink(step - 3)
-            if step >= 7 and step % HALVES == 1:
-                pick((step - 7) // HALVES)
-            if step == 15 + 2:
+        def deal_wc(n):
+            b, i = divmod(n, PACK)
+            wc_q[n] = keep.tile([P, PASSES, P], U32, name="wc_q", tag="wc_q%d" % (n % 2), align_bytes=64)
+            nc.scalar.copy(wc_q[n][:], wc_raw[:, :, b * BANK + i : (b + 1) * BANK : PACK])
+
+        picks_at = {last_piece[TILES - 1] - 2 * (TILES - 1 - n) + PICK_LAG: n for n in range(TILES)}
+        for k in range(max(picks_at) + 1):
+            if k == WC_PIECE:
+                nc.gpsimd.tensor_copy(
+                    wc_s[:].rearrange("p (b i m) -> p b i m", b=PASSES, i=PACK),
+                    wc_s_raw[:].rearrange("p (b m i) -> p b i m", b=PASSES, i=PACK),
+                )
+                deal_wc(0)
+                deal_wc(1)
+            if k < len(pieces):
+                products(k)
+            if 0 <= k - TANH_LAG < len(pieces):
+                bend(k - TANH_LAG)
+            if 0 <= k - SUM_LAG < len(pieces):
+                add_ink(k - SUM_LAG)
+            if k in picks_at:
+                pick(picks_at[k])
+            if k - TANH_LAG == len(pieces) - 1:
                 quantise_x(0)
         quantise_x(1)
 
-        wc_s = keep.tile([P, H], U8, name="wc_s", tag="slot1", align_bytes=64)
-        nc.gpsimd.tensor_copy(
-            wc_s[:].rearrange("p (b i m) -> p b i m", b=PASSES, i=PACK),
-            wc_s_raw[:].rearrange("p (b m i) -> p b i m", b=PASSES, i=PACK),
-        )
         out_v = out.rearrange("(b p i) j -> b i p j", p=P, i=PACK)
-        larger, page = {}, {}
+        page_tags = ("bent%d" % ((len(pieces) - 2) % TANH_BUFFERS), "x_rows1", "x_woven1")
 
-        def second_stage(n):
+        def fill_page(n):
             b, i = divmod(n, PACK)
-            wc_q = keep.tile([P, PASSES, P], U32, name="wc_q", tag=WC_TAGS[n % 2], align_bytes=64)
-            nc.scalar.copy(wc_q[:], wc_raw[:, :, b * BANK + i : (b + 1) * BANK : PACK])
-            page[n] = keep.tile([P, S], F32, name="page", tag=PAGE_TAGS[n % 3], align_bytes=64)
+            page[n] = keep.tile([P, S], F32, name="page", tag=page_tags[n % len(page_tags)], align_bytes=64)
             if n == 0:
                 nc.gpsimd.tensor_scalar(page[n][:], u[n][:], gain_sb[:, b, i : i + 1], skip_sb[:, b, i : i + 1], ALU.mult, ALU.mult)
             else:
                 nc.scalar.activation(page[n][:], u[n][:], ACT.Copy, scale=gain_sb[:, b, i : i + 1])
                 nc.scalar.activation(page[n][:], page[n][:], ACT.Copy, scale=skip_sb[:, b, i : i + 1])
-            y = psum.tile([P, NP], F32, name="y", tag="grain")
+
+        def put(n, cols):
+            b, i = divmod(n, PACK)
+            width = cols.stop - cols.start
+            y = psum.tile([P, width], F32, name="y", tag="grain")
             for a in range(PASSES):
                 nc.tensor.matmul_mx(
-                    out=y[:], lhsT=wc_q[:, a, :].bitcast(FP8X4),
-                    lhsT_scale=wc_s[4 * a :, n * P : (n + 1) * P],
-                    rhs=x_q[a][:].bitcast(FP8X4), rhs_scale=x_s[a][:], start=(a == 0), stop=(a == PASSES - 1),
+                    out=y[:], lhsT=wc_q[n][:, a, :].bitcast(FP8X4), lhsT_scale=wc_s[4 * a :, n * P : (n + 1) * P],
+                    rhs=x_q[a][:, cols].bitcast(FP8X4), rhs_scale=x_s[a][:, cols], start=(a == 0), stop=(a == PASSES - 1),
                 )
-            larger[n] = ring.tile([P, NP], F32, name="larger")
-            nc.vector.tensor_tensor(larger[n][:], y[:], proof_sb[b][:, i, :], ALU.max)
+            larger = ring.tile([P, width], F32, name="larger")
+            nc.vector.tensor_tensor(larger[:], y[:], proof_sb[b][:, i, cols], ALU.max)
+            nc.vector.tensor_tensor(page[n][:].indirect(offsets(pos_sb, cols)), larger[:], wgo_sb[:, i, cols], ALU.mult)
 
-        def put(n):
-            b, i = divmod(n, PACK)
-            nc.vector.tensor_tensor(page[n][:].indirect(pos_sb[:]), larger[n][:], wgo_sb[:, i, :], ALU.mult)
-            nc.sync.dma_start(out_v[b, i], page[n][:])
-
-        for n in range(TILES + 1):
-            if n < TILES:
-                second_stage(n)
-            if n >= 1:
-                put(n - 1)
+        for n in range(TILES):
+            if n not in wc_q:
+                deal_wc(n)
+            fill_page(n)
+            every = slice(0, PICKED)
+            for cols in halves(every) if n == 0 else [every]:
+                put(n, cols)
+            nc.sync.dma_start(out_v[n // PACK, n % PACK], page[n][:])

from contextlib import ExitStack

import concourse.mybir as mybir

K, H, T, S, PICKED = 512, 1024, 4096, 1024, 512
FLOPS = 2 * (2 * K * H * S + H * H * PICKED)

F32 = mybir.dt.float32
BF16 = mybir.dt.bfloat16
I32 = mybir.dt.int32
U32 = mybir.dt.uint32
U16 = mybir.dt.uint16
U8 = mybir.dt.uint8
FP8X4 = mybir.dt.float8_e4m3fn_x4
FP4X4 = mybir.dt.float4_e2m1fn_x4
ALU = mybir.AluOpType
ACT = mybir.ActivationFunctionType

P = 128
PACK = 4
QUADRANTS = 4
LIST_ROWS = 16
BANK = 512
PASSES = H // BANK
TILES = PASSES * PACK
TANH_BUFFERS = 3
TANH_LAG, SUM_LAG = 2, 3
PICK_LAG = 6
WC_PIECE = 9


def offsets(list_tile, cols):
    return list_tile[:, cols.start // LIST_ROWS : cols.stop // LIST_ROWS]


def halves(cols):
    middle = (cols.start + cols.stop) // 2
    return [slice(cols.start, middle), slice(middle, cols.stop)]


def tile_list_stone_wear_watch_kernel(
    tc, tab_words, tab_scales, offs, pos1, wa, wb_words, wb_scales, gain,
    wc_words, wc_scales, proof, skip, wgo, out,
):
    nc = tc.nc
    with ExitStack() as ctx:
        keep = ctx.enter_context(tc.tile_pool(name="keep", bufs=1))
        ring = ctx.enter_context(tc.tile_pool(name="ring", bufs=3))
        psum = ctx.enter_context(tc.psum_pool(name="psum", bufs=4))

        offs_sb = keep.tile([P, S // LIST_ROWS], U16, name="offs_sb")
        pos_sb = keep.tile([P, PICKED // LIST_ROWS], U16, name="pos_sb")
        tab_w = keep.tile([P, T], U32, name="tab_w", align_bytes=64)
        tab_s = keep.tile([P, T], U8, name="tab_s", align_bytes=64)
        wb_s_raw = keep.tile([P, H], U8, name="wb_s_raw", align_bytes=64)
        wb_raw = keep.tile([P, 2 * H], U8, name="wb_raw", align_bytes=64)
        first_pass, second_pass = halves(slice(0, H))
        wa_first = [keep.tile([P, PACK, BANK // 2], F32, name="wa_first%d" % h, align_bytes=64) for h in range(2)]
        wa_second = keep.tile([P, PACK, BANK], F32, name="wa_second")
        wc_raw = keep.tile([P, PASSES, H], U32, name="wc_raw")
        gain_sb = keep.tile([P, PASSES, PACK], F32, name="gain_sb")
        skip_sb = keep.tile([P, PASSES, PACK], F32, name="skip_sb")
        proof_sb = [keep.tile([P, PACK, PICKED], F32, name="proof_sb%d" % b) for b in range(PASSES)]
        wgo_sb = keep.tile([P, PACK, PICKED], F32, name="wgo_sb")
        wc_s_raw = keep.tile([P, H], U8, name="wc_s_raw", align_bytes=64)

        nc.vector.memset(tab_s[:].bitcast(I32), 0)
        nc.gpsimd.memset(wb_s_raw[:].bitcast(I32), 0)
        nc.gpsimd.memset(wc_s_raw[:].bitcast(I32), 0)

        wa_v = wa.rearrange("(p t) c -> p t c", t=PACK)
        nc.sync.dma_start(offs_sb[:], offs)
        nc.sync.dma_start(wa_first[0][:], wa_v[:, :, halves(first_pass)[0]])
        for q in range(QUADRANTS):
            nc.sync.dma_start(tab_s[32 * q : 32 * q + 4, :].bitcast(I32), tab_scales[0, 4 * q : 4 * q + 4, :].bitcast(I32))
        nc.sync.dma_start(wa_first[1][:], wa_v[:, :, halves(first_pass)[1]])
        nc.sync.dma_start(wb_raw[:].bitcast(I32), wb_words[0].bitcast(I32))
        for q in range(QUADRANTS):
            nc.sync.dma_start(wb_s_raw[32 * q : 32 * q + 4, :].bitcast(I32), wb_scales[0, 4 * q : 4 * q + 4, :].bitcast(I32))
        nc.sync.dma_start(tab_w[:].bitcast(I32), tab_words[0].rearrange("p t i -> p (t i)").bitcast(I32))
        nc.sync.dma_start(wa_second[:], wa_v[:, :, second_pass])
        nc.sync.dma_start(pos_sb[:], pos1)
        nc.sync.dma_start(gain_sb[:], gain.rearrange("(b p i) -> p b i", p=P, i=PACK))
        for q in range(QUADRANTS):
            nc.sync.dma_start(wc_s_raw[32 * q : 32 * q + 8, :].bitcast(I32), wc_scales[:, 4 * q : 4 * q + 4, :].bitcast(I32))
        nc.sync.dma_start(skip_sb[:], skip.rearrange("(b p i) -> p b i", p=P, i=PACK))
        nc.sync.dma_start(wc_raw[:].bitcast(I32), wc_words.rearrange("a p c i -> p a (c i)").bitcast(I32))
        proof_v = proof.rearrange("(b p i) m -> b p i m", p=P, i=PACK)
        nc.sync.dma_start(proof_sb[0][:], proof_v[0])
        wgo_v = wgo.rearrange("(q i) m -> q i m", i=PACK)
        for q in range(QUADRANTS):
            nc.sync.dma_start(wgo_sb[32 * q : 32 * q + 32], wgo_v)
        nc.sync.dma_start(proof_sb[1][:], proof_v[1])

        v_s = keep.tile([P, S], U8, name="v_s", align_bytes=64)
        nc.vector.tensor_copy(v_s[:], tab_s[:].indirect(offs_sb[:]))

        left, right = halves(slice(0, S))
        v_q = [keep.tile([P, BANK], U32, name="v_q%d" % bank, align_bytes=64) for bank in range(S // BANK)]
        for cols in halves(left):
            nc.vector.tensor_copy(v_q[0][:, cols], tab_w[:].indirect(offsets(offs_sb, cols)))
        nc.vector.tensor_copy(v_q[1][:], tab_w[:].indirect(offsets(offs_sb, right)))

        wa_q, wa_s = [], []

        def quantise_wa(b):
            grouped = keep.tile([P, PACK * P * PACK], BF16, name="wa_grouped%d" % b, align_bytes=64)
            dst = grouped[:].rearrange("p (i m t) -> p m i t", i=PACK, t=PACK)
            codes = keep.tile([P, BANK], U32, name="wa_q%d" % b, align_bytes=64)
            scales = keep.tile([P, BANK], U8, name="wa_s%d" % b, align_bytes=64)
            if b == 0:
                for raw, places in zip(wa_first, halves(slice(0, P))):
                    nc.scalar.activation(dst[:, places], raw[:].rearrange("p t (m i) -> p m i t", i=PACK), ACT.Copy)
            else:
                nc.vector.tensor_copy(dst, wa_second[:].rearrange("p t (m i) -> p m i t", i=PACK))
            nc.vector.quantize_mx(out=codes[:].bitcast(FP8X4), scales=scales[:], in_=grouped[:])
            wa_q.append(codes)
            wa_s.append(scales)

        quantise_wa(0)

        wb_q = keep.tile([P, 2 * H], U8, name="wb_q", align_bytes=64)
        for b in range(PASSES):
            nc.scalar.copy(
                wb_q[:, b * H : (b + 1) * H].bitcast(U16).rearrange("p (i m) -> p i m", i=PACK),
                wb_raw[:, b * H : (b + 1) * H].bitcast(U16).rearrange("p (m i) -> p i m", i=PACK),
            )
        wb_s = [keep.tile([P, BANK], U8, name="wb_s%d" % b, align_bytes=64) for b in range(PASSES)]
        for b in range(PASSES):
            nc.vector.tensor_copy(
                wb_s[b][:].rearrange("p (i m) -> p i m", i=PACK),
                wb_s_raw[:, b * BANK : (b + 1) * BANK].rearrange("p (m i) -> p i m", i=PACK),
            )

        quantise_wa(1)

        u = [keep.tile([P, S], F32, name="u%d" % n) for n in range(TILES)]
        x_rows = [keep.tile([P, PACK, PICKED], BF16, name="x_rows", tag="x_rows%d" % b, align_bytes=64) for b in range(PASSES)]
        wc_s = keep.tile([P, H], U8, name="wc_s", align_bytes=64)

        pieces = [(0, cols) for cols in halves(left)] + [(1, left), (0, right), (1, right)]
        pieces.extend((n, cols) for n in range(2, TILES) for cols in (left, right))
        last_piece = {n: k for k, (n, cols) in enumerate(pieces)}
        ink, product, bent, x_q, x_s, wc_q, page = {}, {}, {}, [], [], {}, {}

        def products(k):
            n, cols = pieces[k]
            b, i = divmod(n, PACK)
            width = cols.stop - cols.start
            bank = cols.start // BANK
            moving = v_q[bank][:, cols.start - bank * BANK : cols.stop - bank * BANK].bitcast(FP8X4)
            place = slice(i * P, (i + 1) * P)
            ink[k] = psum.tile([P, width], F32, name="ink")
            grain = psum.tile([P, width], F32, name="grain")
            nc.tensor.matmul_mx(
                out=ink[k][:], lhsT=wa_q[b][:, place].bitcast(FP8X4), lhsT_scale=wa_s[b][:, place],
                rhs=moving, rhs_scale=v_s[:, cols], start=True, stop=True,
            )
            nc.tensor.matmul_mx(
                out=grain[:], lhsT=wb_q[:, 2 * n * P : 2 * (n + 1) * P].bitcast(FP4X4), lhsT_scale=wb_s[b][:, place],
                rhs=moving, rhs_scale=v_s[:, cols], start=True, stop=True,
            )
            nc.scalar.copy(u[n][:, cols], ink[k][:])
            product[k] = keep.tile([P, width], F32, name="product", tag="product%d" % k, align_bytes=64)
            nc.vector.tensor_tensor(product[k][:], grain[:], u[n][:, cols], ALU.mult)

        def bend(k):
            n, cols = pieces[k]
            bent[k] = keep.tile([P, cols.stop - cols.start], F32, name="bent", tag="bent%d" % (k % TANH_BUFFERS), align_bytes=64)
            nc.scalar.activation(bent[k][:], product[k][:], ACT.Tanh)

        def add_ink(k):
            n, cols = pieces[k]
            if cols == right and (n % 2 == 0 or n == TILES - 1):
                nc.vector.tensor_tensor(u[n][:, cols], ink[k][:], bent[k][:], ALU.add)
            else:
                nc.gpsimd.tensor_tensor(u[n][:, cols], u[n][:, cols], bent[k][:], ALU.add)

        def pick(n):
            b, i = divmod(n, PACK)
            every = slice(0, PICKED)
            for part, cols in enumerate(halves(every) if n == TILES - 1 else [every]):
                picked = keep.tile([P, cols.stop - cols.start], F32, name="picked", tag="product%d" % (2 * n + 3 + part), align_bytes=64)
                nc.vector.tensor_copy(picked[:], u[n][:].indirect(offsets(pos_sb, cols)))
                if n % 2 == 1 and n < TILES - 1:
                    nc.gpsimd.tensor_scalar(x_rows[b][:, i, cols], picked[:], gain_sb[:, b, i : i + 1], 0.0, ALU.mult, ALU.add)
                else:
                    nc.scalar.activation(x_rows[b][:, i, cols], picked[:], ACT.Copy, scale=gain_sb[:, b, i : i + 1])

        def quantise_x(b):
            codes = keep.tile([P, PICKED], U32, name="x_q%d" % b, align_bytes=64)
            scales = keep.tile([P, PICKED], U8, name="x_s%d" % b, align_bytes=64)
            for part, cols in enumerate(halves(slice(0, PICKED))):
                tag = "product%d" % last_piece[TILES - 2 + part] if b == 0 else "x_woven%d" % part
                woven = keep.tile([P, (cols.stop - cols.start) * PACK], BF16, name="x_woven", tag=tag, align_bytes=64)
                dst = woven[:].rearrange("p (c e i) -> p c i e", e=4, i=PACK)
                src = x_rows[b][:, :, cols].rearrange("p i (c e) -> p c i e", e=4)
                if b == PASSES - 1 and part == 0:
                    nc.vector.tensor_copy(dst, src)
                else:
                    nc.scalar.copy(dst, src)
                nc.vector.quantize_mx(out=codes[:, cols].bitcast(FP8X4), scales=scales[:, cols], in_=woven[:])
            x_q.append(codes)
            x_s.append(scales)

        def deal_wc(n):
            b, i = divmod(n, PACK)
            wc_q[n] = keep.tile([P, PASSES, P], U32, name="wc_q", tag="wc_q%d" % (n % 2), align_bytes=64)
            nc.scalar.copy(wc_q[n][:], wc_raw[:, :, b * BANK + i : (b + 1) * BANK : PACK])

        picks_at = {last_piece[TILES - 1] - 2 * (TILES - 1 - n) + PICK_LAG: n for n in range(TILES)}
        for k in range(max(picks_at) + 1):
            if k == WC_PIECE:
                nc.gpsimd.tensor_copy(
                    wc_s[:].rearrange("p (b i m) -> p b i m", b=PASSES, i=PACK),
                    wc_s_raw[:].rearrange("p (b m i) -> p b i m", b=PASSES, i=PACK),
                )
                deal_wc(0)
                deal_wc(1)
            if k < len(pieces):
                products(k)
            if 0 <= k - TANH_LAG < len(pieces):
                bend(k - TANH_LAG)
            if 0 <= k - SUM_LAG < len(pieces):
                add_ink(k - SUM_LAG)
            if k in picks_at:
                pick(picks_at[k])
            if k - TANH_LAG == len(pieces) - 1:
                quantise_x(0)
        quantise_x(1)

        out_v = out.rearrange("(b p i) j -> b i p j", p=P, i=PACK)
        page_tags = ("bent%d" % ((len(pieces) - 2) % TANH_BUFFERS), "x_rows1", "x_woven1")

        def fill_page(n):
            b, i = divmod(n, PACK)
            page[n] = keep.tile([P, S], F32, name="page", tag=page_tags[n % len(page_tags)], align_bytes=64)
            if n == 0:
                nc.gpsimd.tensor_scalar(page[n][:], u[n][:], gain_sb[:, b, i : i + 1], skip_sb[:, b, i : i + 1], ALU.mult, ALU.mult)
            else:
                nc.scalar.activation(page[n][:], u[n][:], ACT.Copy, scale=gain_sb[:, b, i : i + 1])
                nc.scalar.activation(page[n][:], page[n][:], ACT.Copy, scale=skip_sb[:, b, i : i + 1])

        def put(n, cols):
            b, i = divmod(n, PACK)
            width = cols.stop - cols.start
            y = psum.tile([P, width], F32, name="y", tag="grain")
            for a in range(PASSES):
                nc.tensor.matmul_mx(
                    out=y[:], lhsT=wc_q[n][:, a, :].bitcast(FP8X4), lhsT_scale=wc_s[4 * a :, n * P : (n + 1) * P],
                    rhs=x_q[a][:, cols].bitcast(FP8X4), rhs_scale=x_s[a][:, cols], start=(a == 0), stop=(a == PASSES - 1),
                )
            larger = ring.tile([P, width], F32, name="larger")
            nc.vector.tensor_tensor(larger[:], y[:], proof_sb[b][:, i, cols], ALU.max)
            nc.vector.tensor_tensor(page[n][:].indirect(offsets(pos_sb, cols)), larger[:], wgo_sb[:, i, cols], ALU.mult)

        for n in range(TILES):
            if n not in wc_q:
                deal_wc(n)
            fill_page(n)
            every = slice(0, PICKED)
            for cols in halves(every) if n == 0 else [every]:
                put(n, cols)
            nc.sync.dma_start(out_v[n // PACK, n % PACK], page[n][:])
